import numpy as np
import ml_dtypes


def mxq(x, axis, fmt="e4m3"):
    dtype, down = {"e4m3": (ml_dtypes.float8_e4m3fn, 7), "e5m2": (ml_dtypes.float8_e5m2, 14)}[fmt]
    v = np.moveaxis(np.asarray(x, np.float32).astype(ml_dtypes.bfloat16).astype(np.float64), axis, -1)
    blocks = v.reshape(v.shape[:-1] + (-1, 32))
    amax = np.abs(blocks).max(-1, keepdims=True)
    byte = np.maximum(np.where(amax > 0, np.frexp(amax)[1] - 1 + 127, 0) - down, 1)
    scale = np.exp2(byte - 127.0)
    codes = (blocks / scale).astype(np.float32).astype(dtype).astype(np.float64)
    return np.moveaxis((codes * scale).reshape(v.shape), -1, axis)


WIDE = False


def mx_kscale(k):
    if not WIDE:
        return np.ones(k)
    levels = np.array([10, -10, 5, -5, 0])
    if k % 512:
        return np.exp2(np.random.permutation(np.resize(levels, k // 32))).repeat(32)
    a = np.empty((k // 512, 16))
    for p in range(k // 512):
        a[p, :8] = np.random.permutation(np.resize(levels, 8))
        for g in range(8):
            far = levels[np.abs(levels - a[p, g]) >= 10]
            a[p, g + 8] = far[np.random.randint(len(far))]
    return np.exp2(a.ravel()).repeat(32)


def f64(x):
    return np.asarray(x).astype(np.float64)


def striped(idx):
    return np.tile(idx.reshape(-1, 16).T, (8, 1)).astype(np.uint16)


def unstriped(offs):
    return offs[:16].T.reshape(-1).astype(np.int64)


def striped8(idx):
    return np.concatenate([x.reshape(-1, 16).T for x in idx]).astype(np.uint16)


def runs(offs, k):
    lists = np.stack([offs[16 * r : 16 * r + 16].T.reshape(-1) for r in range(8)]).astype(np.int64)
    return lists[np.arange(k) % 512 // 64]


def pack_weight(w):
    k, n = w.shape
    w = f64(np.asarray(w, np.float32).astype(ml_dtypes.bfloat16)).reshape(k // 32, 32, n)
    amax = np.abs(w).max(1)
    byte = np.clip(np.where(amax > 0, np.frexp(amax)[1] - 1 + 127 - 7, 1), 1, 254)
    scaled = (w * np.exp2(127.0 - byte)[:, None, :]).reshape(k, n).astype(np.float32)
    words = np.ascontiguousarray(scaled.reshape(k // 512, 128, 4, n).transpose(0, 1, 3, 2)).astype(ml_dtypes.float8_e4m3fn).view(np.uint8)
    return words, np.ascontiguousarray(byte.astype(np.uint8).reshape(k // 512, 16, n))


def unpack_weight(words, scales):
    g, p, n, _ = words.shape
    vals = np.ascontiguousarray(words).view(ml_dtypes.float8_e4m3fn).astype(np.float64) * np.repeat(np.exp2(scales.astype(np.float64) - 127.0), 8, axis=1)[..., None]
    return vals.transpose(0, 1, 3, 2).reshape(g * 512, n)


E2M1 = np.array([0.0, 0.5, 1.0, 1.5, 2.0, 3.0, 4.0, 6.0, -0.0, -0.5, -1.0, -1.5, -2.0, -3.0, -4.0, -6.0])


def pack_fp4(w):
    k, n = w.shape
    w = f64(np.asarray(w, np.float32).astype(ml_dtypes.bfloat16)).reshape(k // 32, 32, n)
    amax = np.abs(w).max(1)
    mant, ex = np.frexp(amax / 6.0)
    byte = np.clip(np.where(amax > 0, np.where(mant > 0.5, ex, ex - 1) + 127, 1), 1, 254)
    scaled = (w * np.exp2(127.0 - byte)[:, None, :]).reshape(k, n).astype(np.float32)
    c = np.ascontiguousarray(scaled.reshape(k // 512, 128, 4, n).transpose(0, 1, 3, 2)).astype(ml_dtypes.float4_e2m1fn).view(np.uint8) & 0xF
    words = (c[..., 0::2] | (c[..., 1::2] << 4)).reshape(k // 512, 128, 2 * n)
    return np.ascontiguousarray(words), np.ascontiguousarray(byte.astype(np.uint8).reshape(k // 512, 16, n))


def unpack_fp4(words, scales):
    g, _, n = scales.shape
    words = np.ascontiguousarray(words).reshape(g, 128, n, 2)
    nib = np.empty((g, 128, n, 4), np.uint8)
    nib[..., 0::2] = words & 0xF
    nib[..., 1::2] = words >> 4
    vals = E2M1[nib] * np.repeat(np.exp2(scales.astype(np.float64) - 127.0), 8, axis=1)[..., None]
    return vals.transpose(0, 1, 3, 2).reshape(g * 512, n)


def planes(y):
    n, m = y.shape
    v = y.astype(np.float32).astype(ml_dtypes.bfloat16).astype(np.float64).reshape(n // 32, 32, m)
    top = np.abs(v).max(1)
    byte = np.clip(np.where(top > 0, np.frexp(top)[1] - 1 + 127 - 7, 1), 1, 254)
    codes = (v * np.exp2(127.0 - byte)[:, None, :]).reshape(n, m).astype(np.float32).astype(ml_dtypes.float8_e4m3fn).view(np.uint8)
    words = codes.reshape(n // 512, 128, 4, m).transpose(0, 1, 3, 2)
    return np.ascontiguousarray(words), np.ascontiguousarray(byte.astype(np.uint8).reshape(n // 512, 16, m))


K, T, S, N, H = 512, 2048, 512, 512, 512


def setup_inputs():
    n = np.random.standard_normal
    s = mx_kscale(K)[:, None]
    u = mx_kscale(S)
    packed_xT = pack_weight(n((K, T)) * s)
    packed_w1 = pack_fp4(n((S, N)) / np.sqrt(S) / u[:, None])
    return {
        "x_words": packed_xT[0],
        "x_scales": packed_xT[1],
        "wa": (n((K, H)) / np.sqrt(K) / s).astype(np.float32),
        "gt": (np.random.uniform(0.5, 1.5, (S, 1)) * u[:, None]).astype(np.float32),
        "w1_words": packed_w1[0],
        "w1_scales": packed_w1[1],
        "offs": striped(np.random.permutation(T)[:S]),
        "n1": striped8(np.stack([np.random.permutation(H) for _ in range(8)])),
        "n2": striped8(np.stack([np.random.permutation(H) for _ in range(8)])),
        "n3": striped8(np.stack([np.random.permutation(H) for _ in range(8)])),
        "n4": striped8(np.stack([np.random.permutation(H) for _ in range(8)])),
        "n5": striped8(np.stack([np.random.permutation(H) for _ in range(8)])),
    }


def reference(x_words, x_scales, wa, gt, w1_words, w1_scales, offs, n1, n2, n3, n4, n5):
    xq = unpack_weight(x_words, x_scales)[:, unstriped(offs)]
    y = xq.T @ mxq(f64(wa), 0, "e4m3")
    z = f64(gt) * (y + y[np.arange(S)[:, None], runs(n1, S)] - (np.maximum(y[np.arange(S)[:, None], runs(n2, S)], y[np.arange(S)[:, None], runs(n3, S)])))
    h = unpack_fp4(w1_words, w1_scales).T @ mxq(z, 0, "e4m3")
    st = np.maximum(h, h[np.arange(N)[:, None], runs(n4, N)])
    out_0 = np.minimum(st, st[np.arange(N)[:, None], runs(n5, N)])
    return (out_0,) + planes(out_0)

@@ -1,0 +1,247 @@
+from contextlib import ExitStack
+
+import concourse.mybir as mybir
+
+K, T, S, N, H = 512, 2048, 512, 512, 512
+FLOPS = 2 * K * S * H + 2 * S * N * H
+
+F32 = mybir.dt.float32
+BF16 = mybir.dt.bfloat16
+I32 = mybir.dt.int32
+U32 = mybir.dt.uint32
+U16 = mybir.dt.uint16
+U8 = mybir.dt.uint8
+FP8X4 = mybir.dt.float8_e4m3fn_x4
+FP4X4 = mybir.dt.float4_e2m1fn_x4
+ALU = mybir.AluOpType
+COPY = mybir.ActivationFunctionType.Copy
+
+P = 128
+PACK = 4
+LAST = PACK - 1
+PIECES = ((0, 256), (256, 384), (384, 512))
+
+
+def tile_picked_toktrimhopmn_none_po_kernel(
+    tc, x_words, x_scales, wa, gt, w1_words, w1_scales, offs, n1, n2, n3, n4, n5, out_0, out_1, out_2
+):
+    nc = tc.nc
+    with ExitStack() as ctx:
+        lists = ctx.enter_context(tc.tile_pool(name="lists", bufs=1))
+        keep = ctx.enter_context(tc.tile_pool(name="keep", bufs=1))
+        psum = ctx.enter_context(tc.psum_pool(name="psum", bufs=1))
+
+        def list_tile(name):
+            return lists.tile([P, S // 16], U16, name=name)
+
+        offs_sb, n1_sb, n2_sb, n3_sb, n4_sb, n5_sb = (list_tile(nm) for nm in ("offs", "n1", "n2", "n3", "n4", "n5"))
+
+        def tile(name, shape, dtype):
+            return keep.tile(shape, dtype, name=name, align_bytes=64)
+
+        def looked_up(window, lst, lo, hi):
+            return window[:].indirect(lst[:, lo // 16 : hi // 16])
+
+        def load_scale_rows(plane, rows):
+            for q in range(4):
+                nc.sync.dma_start(plane[32 * q : 32 * q + 4, :].bitcast(I32), rows[0][4 * q : 4 * q + 4, :].bitcast(I32))
+
+        xs = tile("xs", [P, T], U8)
+        xw = tile("xw", [P, T], I32)
+        w1s = tile("w1s", [P, N], U8)
+        w1w = tile("w1w", [P, 2 * N], U8)
+        gt_sb = tile("gt_sb", [P, PACK], F32)
+        wa_raw = [tile(f"wa_raw{c}", [P, PACK, hi - lo], F32) for c, (lo, hi) in enumerate(PIECES)]
+        y_win = [tile(f"y_win{t}", [P, H if t == LAST else 2 * H], F32) for t in range(PACK)]
+        h_win = [tile(f"h_win{t}", [P, 2 * H], F32) for t in range(PACK)]
+        st_win = y_win
+
+        nc.vector.memset(xs[:].bitcast(I32), 0)
+        nc.vector.memset(w1s[:].bitcast(I32), 0)
+
+        wa_rows = wa.rearrange("(p j) c -> p j c", j=PACK)
+        load_scale_rows(xs, x_scales)
+        nc.sync.dma_start(offs_sb[:], offs)
+        nc.sync.dma_start(wa_raw[0][:], wa_rows[:, :, 0:256])
+        nc.sync.dma_start(xw[:], x_words[0].rearrange("p c r -> p (c r)").bitcast(I32))
+        nc.sync.dma_start(wa_raw[1][:], wa_rows[:, :, 256:384])
+        nc.sync.dma_start(wa_raw[2][:], wa_rows[:, :, 384:512])
+        nc.sync.dma_start(n2_sb[:], n2)
+        nc.sync.dma_start(n3_sb[:], n3)
+        nc.sync.dma_start(n1_sb[:], n1)
+        nc.sync.dma_start(gt_sb[:], gt.rearrange("(p t) o -> p (t o)", t=PACK))
+        nc.sync.dma_start(w1w[:].bitcast(I32), w1_words[0].bitcast(I32))
+        load_scale_rows(w1s, w1_scales)
+        nc.sync.dma_start(n4_sb[:], n4)
+        nc.sync.dma_start(n5_sb[:], n5)
+
+        for win in y_win[:LAST] + h_win:
+            nc.vector.memset(win[:, H:], 0.0)
+
+        xs_picked = tile("xs_picked", [P, S], U8)
+        xw_picked = tile("xw_picked", [P, S], U32)
+        xs_dealt = tile("xs_dealt", [P, S], U8)
+        xw_dealt = tile("xw_dealt", [P, S], I32)
+        nc.vector.tensor_copy(xs_picked[:], xs[:].indirect(offs_sb[:]))
+        nc.vector.tensor_copy(
+            xs_dealt[:].rearrange("p (t m) -> p t m", t=PACK), xs_picked[:].rearrange("p (m t) -> p t m", t=PACK)
+        )
+
+        wa_bf = [tile(f"wa_bf{c}", [P, hi - lo, PACK], BF16) for c, (lo, hi) in enumerate(PIECES)]
+        wa_q = [tile(f"wa_q{c}", [P, hi - lo], U32) for c, (lo, hi) in enumerate(PIECES)]
+        wa_s = [tile(f"wa_s{c}", [P, hi - lo], U8) for c, (lo, hi) in enumerate(PIECES)]
+
+        def quantize(codes, scales, grouped):
+            nc.vector.quantize_mx(
+                out=codes.bitcast(FP8X4), scales=scales, in_=grouped[:].rearrange("p c j -> p (c j)")
+            )
+
+        nc.vector.tensor_copy(wa_bf[0][:], wa_raw[0][:].rearrange("p j c -> p c j"))
+        quantize(wa_q[0][:], wa_s[0][:], wa_bf[0])
+        nc.vector.tensor_copy(xw_picked[:], xw[:].bitcast(U32).indirect(offs_sb[:]))
+        nc.vector.tensor_copy(
+            xw_dealt[:].rearrange("p (t m) -> p t m", t=PACK),
+            xw_picked[:].bitcast(I32).rearrange("p (m t) -> p t m", t=PACK),
+        )
+        for c in (1, 2):
+            nc.scalar.copy(wa_bf[c][:], wa_raw[c][:].rearrange("p j c -> p c j"))
+            quantize(wa_q[c][:], wa_s[c][:], wa_bf[c])
+
+        y_ps = [psum.tile([P, H], F32, name=f"y_ps{t}") for t in range(PACK)]
+        y_plain = [tile(f"y_plain{t}", [P, H], F32) for t in range(PACK)]
+        for t in range(PACK):
+            cols = slice(t * P, (t + 1) * P)
+            for c, (lo, hi) in enumerate(PIECES):
+                nc.tensor.matmul_mx(
+                    out=y_ps[t][:, lo:hi],
+                    lhsT=xw_dealt[:, cols].bitcast(FP8X4),
+                    lhsT_scale=xs_dealt[:, cols],
+                    rhs=wa_q[c][:].bitcast(FP8X4),
+                    rhs_scale=wa_s[c][:],
+                    start=True,
+                    stop=True,
+                )
+            nc.scalar.copy(y_win[t][:, :H], y_ps[t][:])
+            nc.scalar.copy(y_plain[t][:], y_ps[t][:])
+
+        w1w_dealt = tile("w1w_dealt", [P, 2 * N], U8)
+        w1s_dealt = tile("w1s_dealt", [P, N], U8)
+        nc.vector.tensor_copy(
+            w1w_dealt[:].rearrange("p (t m b) -> p t m b", t=PACK, b=2),
+            w1w[:].rearrange("p (m t b) -> p t m b", t=PACK, b=2),
+        )
+        nc.vector.tensor_copy(
+            w1s_dealt[:].rearrange("p (t m) -> p t m", t=PACK), w1s[:].rearrange("p (m t) -> p t m", t=PACK)
+        )
+
+        d2 = [tile(f"d2_{t}", [P, H], F32) for t in range(PACK)]
+        d3 = [tile(f"d3_{t}", [P, H], F32) for t in range(PACK)]
+        big = [tile(f"big{t}", [P, H], F32) for t in range(PACK)]
+        mix = [tile(f"mix{t}", [P, H], F32) for t in range(PACK)]
+        z_bf = [tile(f"z_bf{c}", [P, hi - lo, PACK], BF16) for c, (lo, hi) in enumerate(PIECES)]
+        z_q = [tile(f"z_q{c}", [P, hi - lo], U32) for c, (lo, hi) in enumerate(PIECES)]
+        z_s = [tile(f"z_s{c}", [P, hi - lo], U8) for c, (lo, hi) in enumerate(PIECES)]
+        h_ps = [psum.tile([P, H], F32, name=f"h_ps{t}") for t in range(PACK)]
+
+        units = [(t, 0, H) for t in range(LAST)] + [(LAST, lo, hi) for lo, hi in PIECES]
+
+        def step_d2(t, lo, hi):
+            nc.vector.tensor_tensor(d2[t][:, lo:hi], looked_up(y_win[t], n2_sb, lo, hi), y_plain[t][:, lo:hi], ALU.subtract)
+
+        def step_d3(t, lo, hi):
+            nc.vector.tensor_tensor(d3[t][:, lo:hi], looked_up(y_win[t], n3_sb, lo, hi), y_plain[t][:, lo:hi], ALU.subtract)
+
+        def step_big(t, lo, hi):
+            nc.vector.tensor_tensor(big[t][:, lo:hi], d2[t][:, lo:hi], d3[t][:, lo:hi], ALU.max)
+
+        def step_mix(t, lo, hi):
+            nc.vector.tensor_tensor(mix[t][:, lo:hi], looked_up(y_win[t], n1_sb, lo, hi), big[t][:, lo:hi], ALU.subtract)
+            for c, (a, b) in enumerate(PIECES):
+                if lo <= a and b <= hi:
+                    nc.scalar.activation(z_bf[c][:, :, t], mix[t][:, a:b], COPY, scale=gt_sb[:, t : t + 1])
+
+        def second_product(c):
+            lo, hi = PIECES[c]
+            quantize(z_q[c][:], z_s[c][:], z_bf[c])
+            for t in range(PACK):
+                nc.tensor.matmul_mx(
+                    out=h_ps[t][:, lo:hi],
+                    lhsT=w1w_dealt[:, 2 * P * t : 2 * P * (t + 1)].bitcast(FP4X4),
+                    lhsT_scale=w1s_dealt[:, P * t : P * (t + 1)],
+                    rhs=z_q[c][:].bitcast(FP8X4),
+                    rhs_scale=z_s[c][:],
+                    start=True,
+                    stop=True,
+                )
+                nc.scalar.copy(h_win[t][:, lo:hi], h_ps[t][:, lo:hi])
+
+        step_d2(*units[0])
+        step_d3(*units[0])
+        for u in range(1, len(units)):
+            step_d2(*units[u])
+            step_big(*units[u - 1])
+            step_d3(*units[u])
+            step_mix(*units[u - 1])
+            if u == len(units) - 1:
+                second_product(0)
+        step_big(*units[-1])
+        step_mix(*units[-1])
+        second_product(1)
+        second_product(2)
+
+        g4 = [tile(f"g4_{t}", [P, H], F32) for t in range(PACK)]
+        g5 = [tile(f"g5_{t}", [P, H], F32) for t in range(PACK)]
+        res = [tile(f"res{t}", [P, H], F32) for t in range(PACK)]
+        o_bf = [tile(f"o_bf{c}", [P, hi - lo, PACK], BF16) for c, (lo, hi) in enumerate(PIECES)]
+        o_q = [tile(f"o_q{c}", [P, hi - lo], U32) for c, (lo, hi) in enumerate(PIECES)]
+        o_s = tile("o_s", [P, H], U8)
+        out_rows = out_0.rearrange("(p t) j -> p t j", t=PACK)
+        out_words = out_1[0].rearrange("p c r -> p (c r)").bitcast(I32)
+
+        def step_g4(t):
+            nc.vector.tensor_copy(g4[t][:], looked_up(h_win[t], n4_sb, 0, H))
+
+        def step_st(t):
+            nc.vector.tensor_tensor(st_win[t][:, :H], h_win[t][:, :H], g4[t][:], ALU.max)
+
+        def step_g5(t, lo, hi):
+            nc.vector.tensor_copy(g5[t][:, lo:hi], looked_up(st_win[t], n5_sb, lo, hi))
+
+        def step_out(t, lo, hi):
+            nc.vector.tensor_tensor(res[t][:, lo:hi], st_win[t][:, lo:hi], g5[t][:, lo:hi], ALU.min)
+            nc.sync.dma_start(out_rows[:, t, lo:hi], res[t][:, lo:hi])
+            for c, (a, b) in enumerate(PIECES):
+                if lo <= a and b <= hi:
+                    nc.scalar.copy(o_bf[c][:, :, t], res[t][:, a:b])
+
+        def planes(c):
+            lo, hi = PIECES[c]
+            quantize(o_q[c][:], o_s[:, lo:hi], o_bf[c])
+            nc.sync.dma_start(out_words[:, lo:hi], o_q[c][:].bitcast(I32))
+
+        step_g4(0)
+        step_g4(1)
+        step_st(0)
+        step_st(1)
+        step_g5(*units[0])
+        step_g4(2)
+        step_out(*units[0])
+        step_g5(*units[1])
+        step_st(2)
+        step_g4(3)
+        step_out(*units[1])
+        step_g5(*units[2])
+        step_st(3)
+        step_out(*units[2])
+        step_g5(*units[3])
+        step_g5(*units[4])
+        step_out(*units[3])
+        step_g5(*units[5])
+        step_out(*units[4])
+        step_out(*units[5])
+        planes(0)
+        planes(1)
+        planes(2)
+        for q in range(4):
+            queue = nc.scalar if q % 2 else nc.sync
+            queue.dma_start(out_2[0][4 * q : 4 * q + 4, :].bitcast(I32), o_s[32 * q : 32 * q + 4, :].bitcast(I32))

@@ -20,6 +20,8 @@ P = 128
 PACK = 4
 LAST = PACK - 1
 PIECES = ((0, 256), (256, 384), (384, 512))
+HALVES = ((0, 256), (256, 512))
+BLOCKS = ((0, 128), (128, 256), (256, 384), (384, 512))
 
 
 def tile_picked_toktrimhopmn_none_po_kernel(
@@ -36,15 +38,15 @@ def tile_picked_toktrimhopmn_none_po_kernel(
 
         offs_sb, n1_sb, n2_sb, n3_sb, n4_sb, n5_sb = (list_tile(nm) for nm in ("offs", "n1", "n2", "n3", "n4", "n5"))
 
-        def tile(name, shape, dtype):
-            return keep.tile(shape, dtype, name=name, align_bytes=64)
+        def tile(name, shape, dtype, tag=None):
+            return keep.tile(shape, dtype, name=name, tag=tag or name, align_bytes=64)
 
         def looked_up(window, lst, lo, hi):
             return window[:].indirect(lst[:, lo // 16 : hi // 16])
 
-        def load_scale_rows(plane, rows):
+        def load_scale_rows(queue, plane, rows):
             for q in range(4):
-                nc.sync.dma_start(plane[32 * q : 32 * q + 4, :].bitcast(I32), rows[0][4 * q : 4 * q + 4, :].bitcast(I32))
+                queue.dma_start(plane[32 * q : 32 * q + 4, :].bitcast(I32), rows[0][4 * q : 4 * q + 4, :].bitcast(I32))
 
         xs = tile("xs", [P, T], U8)
         xw = tile("xw", [P, T], I32)
@@ -53,86 +55,106 @@ def tile_picked_toktrimhopmn_none_po_kernel(
         gt_sb = tile("gt_sb", [P, PACK], F32)
         wa_raw = [tile(f"wa_raw{c}", [P, PACK, hi - lo], F32) for c, (lo, hi) in enumerate(PIECES)]
         y_win = [tile(f"y_win{t}", [P, H if t == LAST else 2 * H], F32) for t in range(PACK)]
-        h_win = [tile(f"h_win{t}", [P, 2 * H], F32) for t in range(PACK)]
+        h_win = [tile(f"h_win{t}", [P, H if t == LAST else 2 * H], F32) for t in range(PACK)]
         st_win = y_win
 
-        nc.vector.memset(xs[:].bitcast(I32), 0)
-        nc.vector.memset(w1s[:].bitcast(I32), 0)
+        nc.vector.memset(xs[:, : T // 2].bitcast(I32), 0)
+        nc.gpsimd.memset(xs[:, T // 2 :].bitcast(I32), 0)
+        nc.gpsimd.memset(w1s[:].bitcast(I32), 0)
 
         wa_rows = wa.rearrange("(p j) c -> p j c", j=PACK)
-        load_scale_rows(xs, x_scales)
         nc.sync.dma_start(offs_sb[:], offs)
-        nc.sync.dma_start(wa_raw[0][:], wa_rows[:, :, 0:256])
-        nc.sync.dma_start(xw[:], x_words[0].rearrange("p c r -> p (c r)").bitcast(I32))
-        nc.sync.dma_start(wa_raw[1][:], wa_rows[:, :, 256:384])
-        nc.sync.dma_start(wa_raw[2][:], wa_rows[:, :, 384:512])
+        nc.sync.dma_start(w1w[:].bitcast(I32), w1_words[0].bitcast(I32))
+        load_scale_rows(nc.sync, xs, x_scales)
+        for c, (lo, hi) in enumerate(PIECES):
+            nc.sync.dma_start(wa_raw[c][:], wa_rows[:, :, lo:hi])
+            if c == 0:
+                nc.sync.dma_start(xw[:], x_words[0].rearrange("p c r -> p (c r)").bitcast(I32))
         nc.sync.dma_start(n2_sb[:], n2)
         nc.sync.dma_start(n3_sb[:], n3)
+        load_scale_rows(nc.gpsimd, w1s, w1_scales)
         nc.sync.dma_start(n1_sb[:], n1)
-        nc.sync.dma_start(gt_sb[:], gt.rearrange("(p t) o -> p (t o)", t=PACK))
-        nc.sync.dma_start(w1w[:].bitcast(I32), w1_words[0].bitcast(I32))
-        load_scale_rows(w1s, w1_scales)
+        nc.gpsimd.dma_start(gt_sb[:], gt.rearrange("(p t) o -> p (t o)", t=PACK))
         nc.sync.dma_start(n4_sb[:], n4)
         nc.sync.dma_start(n5_sb[:], n5)
 
-        for win in y_win[:LAST] + h_win:
+        for win in y_win[:LAST] + h_win[:LAST]:
             nc.vector.memset(win[:, H:], 0.0)
 
         xs_picked = tile("xs_picked", [P, S], U8)
         xw_picked = tile("xw_picked", [P, S], U32)
         xs_dealt = tile("xs_dealt", [P, S], U8)
-        xw_dealt = tile("xw_dealt", [P, S], I32)
-        nc.vector.tensor_copy(xs_picked[:], xs[:].indirect(offs_sb[:]))
-        nc.vector.tensor_copy(
-            xs_dealt[:].rearrange("p (t m) -> p t m", t=PACK), xs_picked[:].rearrange("p (m t) -> p t m", t=PACK)
-        )
-
-        wa_bf = [tile(f"wa_bf{c}", [P, hi - lo, PACK], BF16) for c, (lo, hi) in enumerate(PIECES)]
-        wa_q = [tile(f"wa_q{c}", [P, hi - lo], U32) for c, (lo, hi) in enumerate(PIECES)]
-        wa_s = [tile(f"wa_s{c}", [P, hi - lo], U8) for c, (lo, hi) in enumerate(PIECES)]
+        w1w_dealt = tile("w1w_dealt", [P, 2 * N], U8)
+        wa_bf = [tile(f"wa_bf{c}", [P, P, PACK], BF16) for c in range(4)]
+        wa_q = tile("wa_q", [P, H], U32)
+        wa_s = tile("wa_s", [P, H], U8)
 
         def quantize(codes, scales, grouped):
             nc.vector.quantize_mx(
                 out=codes.bitcast(FP8X4), scales=scales, in_=grouped[:].rearrange("p c j -> p (c j)")
             )
 
-        nc.vector.tensor_copy(wa_bf[0][:], wa_raw[0][:].rearrange("p j c -> p c j"))
-        quantize(wa_q[0][:], wa_s[0][:], wa_bf[0])
-        nc.vector.tensor_copy(xw_picked[:], xw[:].bitcast(U32).indirect(offs_sb[:]))
-        nc.vector.tensor_copy(
-            xw_dealt[:].rearrange("p (t m) -> p t m", t=PACK),
-            xw_picked[:].bitcast(I32).rearrange("p (m t) -> p t m", t=PACK),
-        )
-        for c in (1, 2):
-            nc.scalar.copy(wa_bf[c][:], wa_raw[c][:].rearrange("p j c -> p c j"))
-            quantize(wa_q[c][:], wa_s[c][:], wa_bf[c])
+        def wa_block(c):
+            piece, lo = (0, c * P) if c < 2 else (c - 1, 0)
+            return wa_raw[piece][:, :, lo : lo + P].rearrange("p j c -> p c j")
 
-        y_ps = [psum.tile([P, H], F32, name=f"y_ps{t}") for t in range(PACK)]
-        y_plain = [tile(f"y_plain{t}", [P, H], F32) for t in range(PACK)]
-        for t in range(PACK):
-            cols = slice(t * P, (t + 1) * P)
-            for c, (lo, hi) in enumerate(PIECES):
-                nc.tensor.matmul_mx(
-                    out=y_ps[t][:, lo:hi],
-                    lhsT=xw_dealt[:, cols].bitcast(FP8X4),
-                    lhsT_scale=xs_dealt[:, cols],
-                    rhs=wa_q[c][:].bitcast(FP8X4),
-                    rhs_scale=wa_s[c][:],
-                    start=True,
-                    stop=True,
-                )
-            nc.scalar.copy(y_win[t][:, :H], y_ps[t][:])
-            nc.scalar.copy(y_plain[t][:], y_ps[t][:])
+        def quantize_wa(c):
+            quantize(wa_q[:, c * P : (c + 1) * P], wa_s[:, c * P : (c + 1) * P], wa_bf[c])
 
-        w1w_dealt = tile("w1w_dealt", [P, 2 * N], U8)
-        w1s_dealt = tile("w1s_dealt", [P, N], U8)
         nc.vector.tensor_copy(
             w1w_dealt[:].rearrange("p (t m b) -> p t m b", t=PACK, b=2),
             w1w[:].rearrange("p (m t b) -> p t m b", t=PACK, b=2),
         )
+        nc.vector.tensor_copy(xs_picked[:], xs[:].indirect(offs_sb[:]))
+        for c in range(2):
+            nc.scalar.copy(wa_bf[c][:], wa_block(c))
+        quantize_wa(0)
+        nc.vector.tensor_copy(
+            xs_dealt[:].rearrange("p (t m) -> p t m", t=PACK), xs_picked[:].rearrange("p (m t) -> p t m", t=PACK)
+        )
+        quantize_wa(1)
+        nc.vector.tensor_copy(xw_picked[:], xw[:].bitcast(U32).indirect(offs_sb[:]))
+        for c in range(2, 4):
+            nc.scalar.copy(wa_bf[c][:], wa_block(c))
+        xw_first = tile("xw_first", [P, P], I32, tag="wa_raw1")
+        xw_rest = tile("xw_rest", [P, LAST, P], I32)
+        xw_dealt = [xw_first[:]] + [xw_rest[:, t, :] for t in range(LAST)]
+        picked = xw_picked[:].bitcast(I32).rearrange("p (m t) -> p t m", t=PACK)
+        quantize_wa(2)
+        nc.vector.tensor_copy(xw_first[:], picked[:, 0, :])
+        quantize_wa(3)
+        nc.vector.tensor_copy(xw_rest[:], picked[:, 1:, :])
+
+        y_ps = [psum.tile([P, H], F32, name=f"y_ps{t}") for t in range(PACK)]
+        h_ps = [psum.tile([P, H], F32, name=f"h_ps{t}") for t in range(PACK)]
+        y_plain = [tile(f"y_plain{t}", [P, H], F32) for t in range(PACK)]
+
+        def first_product(t, bank, lo, hi):
+            cols = slice(t * P, (t + 1) * P)
+            nc.tensor.matmul_mx(
+                out=bank[:, lo:hi],
+                lhsT=xw_dealt[t].bitcast(FP8X4),
+                lhsT_scale=xs_dealt[:, cols],
+                rhs=wa_q[:, lo:hi].bitcast(FP8X4),
+                rhs_scale=wa_s[:, lo:hi],
+                start=True,
+                stop=True,
+            )
+            nc.scalar.copy(y_win[t][:, lo:hi], bank[:, lo:hi])
+
+        for bank, (lo, hi) in zip((y_ps[0], h_ps[3], h_ps[2]), PIECES):
+            first_product(0, bank, lo, hi)
+        split = PIECES[2][0]
+        nc.scalar.copy(y_plain[0][:, split:], h_ps[2][:, split:])
+        for t in range(1, PACK):
+            first_product(t, y_ps[t], 0, H)
+            nc.scalar.copy(y_plain[t][:], y_ps[t][:])
+
+        w1s_dealt = tile("w1s_dealt", [P, N], U8, tag="wa_bf3")
         nc.vector.tensor_copy(
             w1s_dealt[:].rearrange("p (t m) -> p t m", t=PACK), w1s[:].rearrange("p (m t) -> p t m", t=PACK)
         )
+        nc.vector.tensor_copy(y_plain[0][:, :split], y_win[0][:, :split])
 
         d2 = [tile(f"d2_{t}", [P, H], F32) for t in range(PACK)]
         d3 = [tile(f"d3_{t}", [P, H], F32) for t in range(PACK)]
@@ -141,9 +163,13 @@ def tile_picked_toktrimhopmn_none_po_kernel(
         z_bf = [tile(f"z_bf{c}", [P, hi - lo, PACK], BF16) for c, (lo, hi) in enumerate(PIECES)]
         z_q = [tile(f"z_q{c}", [P, hi - lo], U32) for c, (lo, hi) in enumerate(PIECES)]
         z_s = [tile(f"z_s{c}", [P, hi - lo], U8) for c, (lo, hi) in enumerate(PIECES)]
-        h_ps = [psum.tile([P, H], F32, name=f"h_ps{t}") for t in range(PACK)]
 
-        units = [(t, 0, H) for t in range(LAST)] + [(LAST, lo, hi) for lo, hi in PIECES]
+        def regroup(grouped, t, lo, hi, src):
+            return [
+                (grouped[c][:, max(a, lo) - a : min(b, hi) - a, t], src[:, max(a, lo) : min(b, hi)])
+                for c, (a, b) in enumerate(PIECES)
+                if max(a, lo) < min(b, hi)
+            ]
 
         def step_d2(t, lo, hi):
             nc.vector.tensor_tensor(d2[t][:, lo:hi], looked_up(y_win[t], n2_sb, lo, hi), y_plain[t][:, lo:hi], ALU.subtract)
@@ -156,16 +182,15 @@ def tile_picked_toktrimhopmn_none_po_kernel(
 
         def step_mix(t, lo, hi):
             nc.vector.tensor_tensor(mix[t][:, lo:hi], looked_up(y_win[t], n1_sb, lo, hi), big[t][:, lo:hi], ALU.subtract)
-            for c, (a, b) in enumerate(PIECES):
-                if lo <= a and b <= hi:
-                    nc.scalar.activation(z_bf[c][:, :, t], mix[t][:, a:b], COPY, scale=gt_sb[:, t : t + 1])
+            for dst, src in regroup(z_bf, t, lo, hi, mix[t]):
+                nc.scalar.activation(dst, src, COPY, scale=gt_sb[:, t : t + 1])
 
         def second_product(c):
             lo, hi = PIECES[c]
             quantize(z_q[c][:], z_s[c][:], z_bf[c])
             for t in range(PACK):
                 nc.tensor.matmul_mx(
-                    out=h_ps[t][:, lo:hi],
+                    out=(y_ps if c == 2 else h_ps)[t][:, lo:hi],
                     lhsT=w1w_dealt[:, 2 * P * t : 2 * P * (t + 1)].bitcast(FP4X4),
                     lhsT_scale=w1s_dealt[:, P * t : P * (t + 1)],
                     rhs=z_q[c][:].bitcast(FP8X4),
@@ -173,75 +198,92 @@ def tile_picked_toktrimhopmn_none_po_kernel(
                     start=True,
                     stop=True,
                 )
-                nc.scalar.copy(h_win[t][:, lo:hi], h_ps[t][:, lo:hi])
 
-        step_d2(*units[0])
-        step_d3(*units[0])
-        for u in range(1, len(units)):
-            step_d2(*units[u])
-            step_big(*units[u - 1])
-            step_d3(*units[u])
-            step_mix(*units[u - 1])
-            if u == len(units) - 1:
-                second_product(0)
-        step_big(*units[-1])
-        step_mix(*units[-1])
-        second_product(1)
-        second_product(2)
+        step_d2(0, 0, H)
+        step_d3(0, 0, H)
+        for t in (1, 2):
+            step_d2(t, 0, H)
+            step_big(t - 1, 0, H)
+            step_d3(t, 0, H)
+            step_mix(t - 1, 0, H)
+        step_d2(LAST, *HALVES[0])
+        step_big(2, 0, H)
+        step_d3(LAST, *HALVES[0])
+        step_mix(2, 0, H)
+        step_d2(LAST, *HALVES[1])
+        step_big(LAST, *HALVES[0])
+        step_d3(LAST, *HALVES[1])
+        step_mix(LAST, *BLOCKS[0])
+        step_big(LAST, *HALVES[1])
+        for block in BLOCKS[1:]:
+            step_mix(LAST, *block)
+        for c in range(3):
+            second_product(c)
+        for t in range(PACK):
+            nc.scalar.copy(h_win[t][:, :split], h_ps[t][:, :split])
+            nc.scalar.copy(h_win[t][:, split:H], y_ps[t][:, split:])
 
         g4 = [tile(f"g4_{t}", [P, H], F32) for t in range(PACK)]
         g5 = [tile(f"g5_{t}", [P, H], F32) for t in range(PACK)]
         res = [tile(f"res{t}", [P, H], F32) for t in range(PACK)]
         o_bf = [tile(f"o_bf{c}", [P, hi - lo, PACK], BF16) for c, (lo, hi) in enumerate(PIECES)]
-        o_q = [tile(f"o_q{c}", [P, hi - lo], U32) for c, (lo, hi) in enumerate(PIECES)]
+        o_q = tile("o_q", [P, H], U32)
         o_s = tile("o_s", [P, H], U8)
         out_rows = out_0.rearrange("(p t) j -> p t j", t=PACK)
         out_words = out_1[0].rearrange("p c r -> p (c r)").bitcast(I32)
 
-        def step_g4(t):
-            nc.vector.tensor_copy(g4[t][:], looked_up(h_win[t], n4_sb, 0, H))
+        def step_g4(t, lo, hi):
+            nc.vector.tensor_copy(g4[t][:, lo:hi], looked_up(h_win[t], n4_sb, lo, hi))
 
-        def step_st(t):
-            nc.vector.tensor_tensor(st_win[t][:, :H], h_win[t][:, :H], g4[t][:], ALU.max)
+        def step_st(t, lo, hi):
+            nc.vector.tensor_tensor(st_win[t][:, lo:hi], h_win[t][:, lo:hi], g4[t][:, lo:hi], ALU.max)
 
         def step_g5(t, lo, hi):
             nc.vector.tensor_copy(g5[t][:, lo:hi], looked_up(st_win[t], n5_sb, lo, hi))
 
         def step_out(t, lo, hi):
             nc.vector.tensor_tensor(res[t][:, lo:hi], st_win[t][:, lo:hi], g5[t][:, lo:hi], ALU.min)
+            for dst, src in regroup(o_bf, t, lo, hi, res[t]):
+                nc.scalar.copy(dst, src)
+
+        def store_out(t, lo, hi):
             nc.sync.dma_start(out_rows[:, t, lo:hi], res[t][:, lo:hi])
-            for c, (a, b) in enumerate(PIECES):
-                if lo <= a and b <= hi:
-                    nc.scalar.copy(o_bf[c][:, :, t], res[t][:, a:b])
 
         def planes(c):
             lo, hi = PIECES[c]
-            quantize(o_q[c][:], o_s[:, lo:hi], o_bf[c])
-            nc.sync.dma_start(out_words[:, lo:hi], o_q[c][:].bitcast(I32))
+            quantize(o_q[:, lo:hi], o_s[:, lo:hi], o_bf[c])
 
-        step_g4(0)
-        step_g4(1)
-        step_st(0)
-        step_st(1)
-        step_g5(*units[0])
-        step_g4(2)
-        step_out(*units[0])
-        step_g5(*units[1])
-        step_st(2)
-        step_g4(3)
-        step_out(*units[1])
-        step_g5(*units[2])
-        step_st(3)
-        step_out(*units[2])
-        step_g5(*units[3])
-        step_g5(*units[4])
-        step_out(*units[3])
-        step_g5(*units[5])
-        step_out(*units[4])
-        step_out(*units[5])
+        step_g4(0, 0, H)
+        step_g4(1, 0, H)
+        step_st(0, 0, H)
+        step_st(1, 0, H)
+        step_g5(0, 0, H)
+        step_g4(2, 0, H)
+        step_out(0, 0, H)
+        store_out(0, 0, H)
+        step_g5(1, 0, H)
+        step_st(2, 0, H)
+        step_out(1, 0, H)
+        store_out(1, 0, H)
+        step_g5(2, 0, H)
+        step_g4(LAST, *HALVES[0])
+        step_out(2, 0, H)
+        store_out(2, 0, H)
+        step_g4(LAST, *HALVES[1])
+        step_st(LAST, *HALVES[0])
+        step_st(LAST, *HALVES[1])
+        step_g5(LAST, *BLOCKS[0])
+        for b in range(1, 4):
+            step_g5(LAST, *BLOCKS[b])
+            step_out(LAST, *BLOCKS[b - 1])
+        store_out(LAST, 0, split)
         planes(0)
+        step_out(LAST, *BLOCKS[3])
+        store_out(LAST, split, H)
         planes(1)
+        nc.sync.dma_start(out_words[:, :split], o_q[:, :split].bitcast(I32))
         planes(2)
+        nc.sync.dma_start(out_words[:, split:], o_q[:, split:].bitcast(I32))
         for q in range(4):
             queue = nc.scalar if q % 2 else nc.sync
             queue.dma_start(out_2[0][4 * q : 4 * q + 4, :].bitcast(I32), o_s[32 * q : 32 * q + 4, :].bitcast(I32))

@@ -44,9 +44,9 @@ def tile_picked_toktrimhopmn_none_po_kernel(
         def looked_up(window, lst, lo, hi):
             return window[:].indirect(lst[:, lo // 16 : hi // 16])
 
-        def load_scale_rows(queue, plane, rows):
+        def load_scale_rows(plane, rows):
             for q in range(4):
-                queue.dma_start(plane[32 * q : 32 * q + 4, :].bitcast(I32), rows[0][4 * q : 4 * q + 4, :].bitcast(I32))
+                nc.sync.dma_start(plane[32 * q : 32 * q + 4, :].bitcast(I32), rows[0][4 * q : 4 * q + 4, :].bitcast(I32))
 
         xs = tile("xs", [P, T], U8)
         xw = tile("xw", [P, T], I32)
@@ -65,21 +65,20 @@ def tile_picked_toktrimhopmn_none_po_kernel(
         wa_rows = wa.rearrange("(p j) c -> p j c", j=PACK)
         nc.sync.dma_start(offs_sb[:], offs)
         nc.sync.dma_start(w1w[:].bitcast(I32), w1_words[0].bitcast(I32))
-        load_scale_rows(nc.sync, xs, x_scales)
+        load_scale_rows(xs, x_scales)
         for c, (lo, hi) in enumerate(PIECES):
             nc.sync.dma_start(wa_raw[c][:], wa_rows[:, :, lo:hi])
             if c == 0:
                 nc.sync.dma_start(xw[:], x_words[0].rearrange("p c r -> p (c r)").bitcast(I32))
+        load_scale_rows(w1s, w1_scales)
         nc.sync.dma_start(n2_sb[:], n2)
         nc.sync.dma_start(n3_sb[:], n3)
-        load_scale_rows(nc.gpsimd, w1s, w1_scales)
         nc.sync.dma_start(n1_sb[:], n1)
-        nc.gpsimd.dma_start(gt_sb[:], gt.rearrange("(p t) o -> p (t o)", t=PACK))
+        nc.sync.dma_start(gt_sb[:], gt.rearrange("(p t) o -> p (t o)", t=PACK))
         nc.sync.dma_start(n4_sb[:], n4)
         nc.sync.dma_start(n5_sb[:], n5)
 
-        for win in y_win[:LAST] + h_win[:LAST]:
-            nc.vector.memset(win[:, H:], 0.0)
+        nc.vector.memset(y_win[0][:, H:], 0.0)
 
         xs_picked = tile("xs_picked", [P, S], U8)
         xw_picked = tile("xw_picked", [P, S], U32)
@@ -116,18 +115,18 @@ def tile_picked_toktrimhopmn_none_po_kernel(
         nc.vector.tensor_copy(xw_picked[:], xw[:].bitcast(U32).indirect(offs_sb[:]))
         for c in range(2, 4):
             nc.scalar.copy(wa_bf[c][:], wa_block(c))
-        xw_first = tile("xw_first", [P, P], I32, tag="wa_raw1")
-        xw_rest = tile("xw_rest", [P, LAST, P], I32)
-        xw_dealt = [xw_first[:]] + [xw_rest[:, t, :] for t in range(LAST)]
+        xw_first = tile("xw_first", [P, 2, P], I32, tag="wa_raw1")
+        xw_rest = tile("xw_rest", [P, 2, P], I32, tag="wa_raw2")
+        xw_dealt = [pair[:, e, :] for pair in (xw_first, xw_rest) for e in range(2)]
         picked = xw_picked[:].bitcast(I32).rearrange("p (m t) -> p t m", t=PACK)
         quantize_wa(2)
-        nc.vector.tensor_copy(xw_first[:], picked[:, 0, :])
+        nc.vector.tensor_copy(xw_first[:], picked[:, :2, :])
         quantize_wa(3)
-        nc.vector.tensor_copy(xw_rest[:], picked[:, 1:, :])
+        nc.vector.tensor_copy(xw_rest[:], picked[:, 2:, :])
 
         y_ps = [psum.tile([P, H], F32, name=f"y_ps{t}") for t in range(PACK)]
         h_ps = [psum.tile([P, H], F32, name=f"h_ps{t}") for t in range(PACK)]
-        y_plain = [tile(f"y_plain{t}", [P, H], F32) for t in range(PACK)]
+        y_plain = [win[:, H:] for win in (y_win[1], y_win[2], h_win[0], h_win[1])]
 
         def first_product(t, bank, lo, hi):
             cols = slice(t * P, (t + 1) * P)
@@ -140,25 +139,29 @@ def tile_picked_toktrimhopmn_none_po_kernel(
                 start=True,
                 stop=True,
             )
-            nc.scalar.copy(y_win[t][:, lo:hi], bank[:, lo:hi])
 
-        for bank, (lo, hi) in zip((y_ps[0], h_ps[3], h_ps[2]), PIECES):
-            first_product(0, bank, lo, hi)
+        half = H // 2
         split = PIECES[2][0]
-        nc.scalar.copy(y_plain[0][:, split:], h_ps[2][:, split:])
+        first_product(0, y_ps[0], 0, half)
+        nc.vector.tensor_copy(y_win[0][:, :half], y_ps[0][:, :half])
+        for bank, (lo, hi) in zip((h_ps[3], h_ps[2]), PIECES[1:]):
+            first_product(0, bank, lo, hi)
+            nc.scalar.copy(y_win[0][:, lo:hi], bank[:, lo:hi])
+            nc.scalar.copy(y_plain[0][:, lo:hi], bank[:, lo:hi])
         for t in range(1, PACK):
             first_product(t, y_ps[t], 0, H)
-            nc.scalar.copy(y_plain[t][:], y_ps[t][:])
+            nc.scalar.copy(y_win[t][:, :H], y_ps[t][:])
+            nc.scalar.copy(y_plain[t], y_ps[t][:])
 
         w1s_dealt = tile("w1s_dealt", [P, N], U8, tag="wa_bf3")
         nc.vector.tensor_copy(
             w1s_dealt[:].rearrange("p (t m) -> p t m", t=PACK), w1s[:].rearrange("p (m t) -> p t m", t=PACK)
         )
-        nc.vector.tensor_copy(y_plain[0][:, :split], y_win[0][:, :split])
+        nc.vector.tensor_copy(y_plain[0][:, :half], y_win[0][:, :half])
 
         d2 = [tile(f"d2_{t}", [P, H], F32) for t in range(PACK)]
         d3 = [tile(f"d3_{t}", [P, H], F32) for t in range(PACK)]
-        big = [tile(f"big{t}", [P, H], F32) for t in range(PACK)]
+        big = [h_win[2][:, H:]] + [tile(f"big{t}", [P, H], F32)[:] for t in range(1, PACK)]
         mix = [tile(f"mix{t}", [P, H], F32) for t in range(PACK)]
         z_bf = [tile(f"z_bf{c}", [P, hi - lo, PACK], BF16) for c, (lo, hi) in enumerate(PIECES)]
         z_q = [tile(f"z_q{c}", [P, hi - lo], U32) for c, (lo, hi) in enumerate(PIECES)]
@@ -225,7 +228,8 @@ def tile_picked_toktrimhopmn_none_po_kernel(
 
         g4 = [tile(f"g4_{t}", [P, H], F32) for t in range(PACK)]
         g5 = [tile(f"g5_{t}", [P, H], F32) for t in range(PACK)]
-        res = [tile(f"res{t}", [P, H], F32) for t in range(PACK)]
+        res_pair = [tile(f"res{u}", [P, 2, H], F32) for u in range(2)]
+        res = [res_pair[t // 2][:, t % 2, :] for t in range(PACK)]
         o_bf = [tile(f"o_bf{c}", [P, hi - lo, PACK], BF16) for c, (lo, hi) in enumerate(PIECES)]
         o_q = tile("o_q", [P, H], U32)
         o_s = tile("o_s", [P, H], U8)
@@ -243,8 +247,14 @@ def tile_picked_toktrimhopmn_none_po_kernel(
 
         def step_out(t, lo, hi):
             nc.vector.tensor_tensor(res[t][:, lo:hi], st_win[t][:, lo:hi], g5[t][:, lo:hi], ALU.min)
-            for dst, src in regroup(o_bf, t, lo, hi, res[t]):
-                nc.scalar.copy(dst, src)
+
+        def round_pair(u, lo, hi):
+            for c, (a, b) in enumerate(PIECES):
+                if max(a, lo) < min(b, hi):
+                    nc.scalar.copy(
+                        o_bf[c][:, max(a, lo) - a : min(b, hi) - a, 2 * u : 2 * u + 2],
+                        res_pair[u][:, :, max(a, lo) : min(b, hi)].rearrange("p e c -> p c e"),
+                    )
 
         def store_out(t, lo, hi):
             nc.sync.dma_start(out_rows[:, t, lo:hi], res[t][:, lo:hi])
@@ -265,21 +275,24 @@ def tile_picked_toktrimhopmn_none_po_kernel(
         step_st(2, 0, H)
         step_out(1, 0, H)
         store_out(1, 0, H)
-        step_g5(2, 0, H)
+        round_pair(0, 0, H)
         step_g4(LAST, *HALVES[0])
-        step_out(2, 0, H)
-        store_out(2, 0, H)
         step_g4(LAST, *HALVES[1])
         step_st(LAST, *HALVES[0])
+        step_g5(2, 0, H)
         step_st(LAST, *HALVES[1])
+        step_out(2, 0, H)
+        store_out(2, 0, H)
         step_g5(LAST, *BLOCKS[0])
         for b in range(1, 4):
             step_g5(LAST, *BLOCKS[b])
             step_out(LAST, *BLOCKS[b - 1])
+            round_pair(1, *BLOCKS[b - 1])
         store_out(LAST, 0, split)
-        planes(0)
         step_out(LAST, *BLOCKS[3])
+        round_pair(1, *BLOCKS[3])
         store_out(LAST, split, H)
+        planes(0)
         planes(1)
         nc.sync.dma_start(out_words[:, :split], o_q[:, :split].bitcast(I32))
         planes(2)

@@ -15,6 +15,7 @@ FP8X4 = mybir.dt.float8_e4m3fn_x4
 FP4X4 = mybir.dt.float4_e2m1fn_x4
 ALU = mybir.AluOpType
 COPY = mybir.ActivationFunctionType.Copy
+RELU = mybir.ActivationFunctionType.Relu
 
 P = 128
 PACK = 4
@@ -56,7 +57,7 @@ def tile_picked_toktrimhopmn_none_po_kernel(
         wa_raw = [tile(f"wa_raw{c}", [P, PACK, hi - lo], F32) for c, (lo, hi) in enumerate(PIECES)]
         y_win = [tile(f"y_win{t}", [P, H if t == LAST else 2 * H], F32) for t in range(PACK)]
         h_win = [tile(f"h_win{t}", [P, H if t == LAST else 2 * H], F32) for t in range(PACK)]
-        st_win = y_win
+        st_win = [y_win[0], y_win[3], y_win[1], y_win[2]]
 
         nc.vector.memset(xs[:, : T // 2].bitcast(I32), 0)
         nc.gpsimd.memset(xs[:, T // 2 :].bitcast(I32), 0)
@@ -193,7 +194,7 @@ def tile_picked_toktrimhopmn_none_po_kernel(
             quantize(z_q[c][:], z_s[c][:], z_bf[c])
             for t in range(PACK):
                 nc.tensor.matmul_mx(
-                    out=(y_ps if c == 2 else h_ps)[t][:, lo:hi],
+                    out=(y_ps if (t, c) == (0, 2) else h_ps)[t][:, lo:hi],
                     lhsT=w1w_dealt[:, 2 * P * t : 2 * P * (t + 1)].bitcast(FP4X4),
                     lhsT_scale=w1s_dealt[:, P * t : P * (t + 1)],
                     rhs=z_q[c][:].bitcast(FP8X4),
@@ -222,9 +223,10 @@ def tile_picked_toktrimhopmn_none_po_kernel(
             step_mix(LAST, *block)
         for c in range(3):
             second_product(c)
-        for t in range(PACK):
-            nc.scalar.copy(h_win[t][:, :split], h_ps[t][:, :split])
-            nc.scalar.copy(h_win[t][:, split:H], y_ps[t][:, split:])
+        nc.scalar.copy(h_win[0][:, :split], h_ps[0][:, :split])
+        nc.scalar.copy(h_win[0][:, split:H], y_ps[0][:, split:])
+        for t in range(1, PACK):
+            nc.scalar.copy(h_win[t][:, :H], h_ps[t][:])
 
         g4 = [tile(f"g4_{t}", [P, H], F32) for t in range(PACK)]
         g5 = [tile(f"g5_{t}", [P, H], F32) for t in range(PACK)]
@@ -239,8 +241,18 @@ def tile_picked_toktrimhopmn_none_po_kernel(
         def step_g4(t, lo, hi):
             nc.vector.tensor_copy(g4[t][:, lo:hi], looked_up(h_win[t], n4_sb, lo, hi))
 
-        def step_st(t, lo, hi):
-            nc.vector.tensor_tensor(st_win[t][:, lo:hi], h_win[t][:, lo:hi], g4[t][:, lo:hi], ALU.max)
+        def step_st(t):
+            nc.vector.tensor_tensor(st_win[t][:, :H], h_ps[t][:], g4[t][:], ALU.max)
+
+        gap = [tile(f"gap{t}", [P, H], F32) for t in range(2)]
+        gain = [tile(f"gain{t}", [P, H], F32) for t in range(2)]
+
+        def step_gain(t):
+            nc.gpsimd.tensor_tensor(gap[t][:], g4[t][:], h_win[t][:, :H], ALU.subtract)
+            nc.scalar.activation(gain[t][:], gap[t][:], RELU)
+
+        def step_raise(t):
+            nc.gpsimd.tensor_tensor(st_win[t][:, :H], h_win[t][:, :H], gain[t][:], ALU.add)
 
         def step_g5(t, lo, hi):
             nc.vector.tensor_copy(g5[t][:, lo:hi], looked_up(st_win[t], n5_sb, lo, hi))
@@ -263,35 +275,35 @@ def tile_picked_toktrimhopmn_none_po_kernel(
             lo, hi = PIECES[c]
             quantize(o_q[:, lo:hi], o_s[:, lo:hi], o_bf[c])
 
-        step_g4(0, 0, H)
-        step_g4(1, 0, H)
-        step_st(0, 0, H)
-        step_st(1, 0, H)
-        step_g5(0, 0, H)
+        for t in range(2):
+            step_g4(t, 0, H)
+            step_gain(t)
+        for t in range(2):
+            step_raise(t)
         step_g4(2, 0, H)
-        step_out(0, 0, H)
-        store_out(0, 0, H)
-        step_g5(1, 0, H)
-        step_st(2, 0, H)
-        step_out(1, 0, H)
-        store_out(1, 0, H)
-        round_pair(0, 0, H)
-        step_g4(LAST, *HALVES[0])
-        step_g4(LAST, *HALVES[1])
-        step_st(LAST, *HALVES[0])
+        step_g4(3, *HALVES[0])
+        step_g4(3, *HALVES[1])
+        step_st(2)
+        step_st(3)
         step_g5(2, 0, H)
-        step_st(LAST, *HALVES[1])
+        step_g5(3, 0, H)
         step_out(2, 0, H)
         store_out(2, 0, H)
-        step_g5(LAST, *BLOCKS[0])
+        step_out(3, 0, H)
+        store_out(3, 0, H)
+        round_pair(1, 0, H)
+        step_g5(0, 0, H)
+        step_g5(1, *BLOCKS[0])
+        step_out(0, 0, H)
+        store_out(0, 0, H)
         for b in range(1, 4):
-            step_g5(LAST, *BLOCKS[b])
-            step_out(LAST, *BLOCKS[b - 1])
-            round_pair(1, *BLOCKS[b - 1])
-        store_out(LAST, 0, split)
-        step_out(LAST, *BLOCKS[3])
-        round_pair(1, *BLOCKS[3])
-        store_out(LAST, split, H)
+            step_g5(1, *BLOCKS[b])
+            step_out(1, *BLOCKS[b - 1])
+            round_pair(0, *BLOCKS[b - 1])
+        store_out(1, 0, split)
+        step_out(1, *BLOCKS[3])
+        round_pair(0, *BLOCKS[3])
+        store_out(1, split, H)
         planes(0)
         planes(1)
         nc.sync.dma_start(out_words[:, :split], o_q[:, :split].bitcast(I32))

from contextlib import ExitStack

import concourse.mybir as mybir

K, T, S, N, H = 512, 2048, 512, 512, 512
FLOPS = 2 * K * S * H + 2 * S * N * H

F32 = mybir.dt.float32
BF16 = mybir.dt.bfloat16
I32 = mybir.dt.int32
U32 = mybir.dt.uint32
U16 = mybir.dt.uint16
U8 = mybir.dt.uint8
FP8X4 = mybir.dt.float8_e4m3fn_x4
FP4X4 = mybir.dt.float4_e2m1fn_x4
ALU = mybir.AluOpType
COPY = mybir.ActivationFunctionType.Copy
RELU = mybir.ActivationFunctionType.Relu

P = 128
PACK = 4
LAST = PACK - 1
PIECES = ((0, 256), (256, 384), (384, 512))
HALVES = ((0, 256), (256, 512))
BLOCKS = ((0, 128), (128, 256), (256, 384), (384, 512))


def tile_picked_toktrimhopmn_none_po_kernel(
    tc, x_words, x_scales, wa, gt, w1_words, w1_scales, offs, n1, n2, n3, n4, n5, out_0, out_1, out_2
):
    nc = tc.nc
    with ExitStack() as ctx:
        lists = ctx.enter_context(tc.tile_pool(name="lists", bufs=1))
        keep = ctx.enter_context(tc.tile_pool(name="keep", bufs=1))
        psum = ctx.enter_context(tc.psum_pool(name="psum", bufs=1))

        def list_tile(name):
            return lists.tile([P, S // 16], U16, name=name)

        offs_sb, n1_sb, n2_sb, n3_sb, n4_sb, n5_sb = (list_tile(nm) for nm in ("offs", "n1", "n2", "n3", "n4", "n5"))

        def tile(name, shape, dtype, tag=None):
            return keep.tile(shape, dtype, name=name, tag=tag or name, align_bytes=64)

        def looked_up(window, lst, lo, hi):
            return window[:].indirect(lst[:, lo // 16 : hi // 16])

        def load_scale_rows(plane, rows):
            for q in range(4):
                nc.sync.dma_start(plane[32 * q : 32 * q + 4, :].bitcast(I32), rows[0][4 * q : 4 * q + 4, :].bitcast(I32))

        xs = tile("xs", [P, T], U8)
        xw = tile("xw", [P, T], I32)
        w1s = tile("w1s", [P, N], U8)
        w1w = tile("w1w", [P, 2 * N], U8)
        gt_sb = tile("gt_sb", [P, PACK], F32)
        wa_raw = [tile(f"wa_raw{c}", [P, PACK, hi - lo], F32) for c, (lo, hi) in enumerate(PIECES)]
        y_win = [tile(f"y_win{t}", [P, H if t == LAST else 2 * H], F32) for t in range(PACK)]
        h_win = [tile(f"h_win{t}", [P, H if t == LAST else 2 * H], F32) for t in range(PACK)]
        st_win = [y_win[0], y_win[3], y_win[1], y_win[2]]

        nc.vector.memset(xs[:, : T // 2].bitcast(I32), 0)
        nc.gpsimd.memset(xs[:, T // 2 :].bitcast(I32), 0)
        nc.gpsimd.memset(w1s[:].bitcast(I32), 0)

        wa_rows = wa.rearrange("(p j) c -> p j c", j=PACK)
        nc.sync.dma_start(offs_sb[:], offs)
        nc.sync.dma_start(w1w[:].bitcast(I32), w1_words[0].bitcast(I32))
        load_scale_rows(xs, x_scales)
        for c, (lo, hi) in enumerate(PIECES):
            nc.sync.dma_start(wa_raw[c][:], wa_rows[:, :, lo:hi])
            if c == 0:
                nc.sync.dma_start(xw[:], x_words[0].rearrange("p c r -> p (c r)").bitcast(I32))
        load_scale_rows(w1s, w1_scales)
        nc.sync.dma_start(n2_sb[:], n2)
        nc.sync.dma_start(n3_sb[:], n3)
        nc.sync.dma_start(n1_sb[:], n1)
        nc.sync.dma_start(gt_sb[:], gt.rearrange("(p t) o -> p (t o)", t=PACK))
        nc.sync.dma_start(n4_sb[:], n4)
        nc.sync.dma_start(n5_sb[:], n5)

        nc.vector.memset(y_win[0][:, H:], 0.0)

        xs_picked = tile("xs_picked", [P, S], U8)
        xw_picked = tile("xw_picked", [P, S], U32)
        xs_dealt = tile("xs_dealt", [P, S], U8)
        w1w_dealt = tile("w1w_dealt", [P, 2 * N], U8)
        wa_bf = [tile(f"wa_bf{c}", [P, P, PACK], BF16) for c in range(4)]
        wa_q = tile("wa_q", [P, H], U32)
        wa_s = tile("wa_s", [P, H], U8)

        def quantize(codes, scales, grouped):
            nc.vector.quantize_mx(
                out=codes.bitcast(FP8X4), scales=scales, in_=grouped[:].rearrange("p c j -> p (c j)")
            )

        def wa_block(c):
            piece, lo = (0, c * P) if c < 2 else (c - 1, 0)
            return wa_raw[piece][:, :, lo : lo + P].rearrange("p j c -> p c j")

        def quantize_wa(c):
            quantize(wa_q[:, c * P : (c + 1) * P], wa_s[:, c * P : (c + 1) * P], wa_bf[c])

        nc.vector.tensor_copy(
            w1w_dealt[:].rearrange("p (t m b) -> p t m b", t=PACK, b=2),
            w1w[:].rearrange("p (m t b) -> p t m b", t=PACK, b=2),
        )
        nc.vector.tensor_copy(xs_picked[:], xs[:].indirect(offs_sb[:]))
        for c in range(2):
            nc.scalar.copy(wa_bf[c][:], wa_block(c))
        quantize_wa(0)
        nc.vector.tensor_copy(
            xs_dealt[:].rearrange("p (t m) -> p t m", t=PACK), xs_picked[:].rearrange("p (m t) -> p t m", t=PACK)
        )
        quantize_wa(1)
        nc.vector.tensor_copy(xw_picked[:], xw[:].bitcast(U32).indirect(offs_sb[:]))
        for c in range(2, 4):
            nc.scalar.copy(wa_bf[c][:], wa_block(c))
        xw_first = tile("xw_first", [P, 2, P], I32, tag="wa_raw1")
        xw_rest = tile("xw_rest", [P, 2, P], I32, tag="wa_raw2")
        xw_dealt = [pair[:, e, :] for pair in (xw_first, xw_rest) for e in range(2)]
        picked = xw_picked[:].bitcast(I32).rearrange("p (m t) -> p t m", t=PACK)
        quantize_wa(2)
        nc.vector.tensor_copy(xw_first[:], picked[:, :2, :])
        quantize_wa(3)
        nc.vector.tensor_copy(xw_rest[:], picked[:, 2:, :])

        y_ps = [psum.tile([P, H], F32, name=f"y_ps{t}") for t in range(PACK)]
        h_ps = [psum.tile([P, H], F32, name=f"h_ps{t}") for t in range(PACK)]
        y_plain = [win[:, H:] for win in (y_win[1], y_win[2], h_win[0], h_win[1])]

        def first_product(t, bank, lo, hi):
            cols = slice(t * P, (t + 1) * P)
            nc.tensor.matmul_mx(
                out=bank[:, lo:hi],
                lhsT=xw_dealt[t].bitcast(FP8X4),
                lhsT_scale=xs_dealt[:, cols],
                rhs=wa_q[:, lo:hi].bitcast(FP8X4),
                rhs_scale=wa_s[:, lo:hi],
                start=True,
                stop=True,
            )

        half = H // 2
        split = PIECES[2][0]
        first_product(0, y_ps[0], 0, half)
        nc.vector.tensor_copy(y_win[0][:, :half], y_ps[0][:, :half])
        for bank, (lo, hi) in zip((h_ps[3], h_ps[2]), PIECES[1:]):
            first_product(0, bank, lo, hi)
            nc.scalar.copy(y_win[0][:, lo:hi], bank[:, lo:hi])
            nc.scalar.copy(y_plain[0][:, lo:hi], bank[:, lo:hi])
        for t in range(1, PACK):
            first_product(t, y_ps[t], 0, H)
            nc.scalar.copy(y_win[t][:, :H], y_ps[t][:])
            nc.scalar.copy(y_plain[t], y_ps[t][:])

        w1s_dealt = tile("w1s_dealt", [P, N], U8, tag="wa_bf3")
        nc.vector.tensor_copy(
            w1s_dealt[:].rearrange("p (t m) -> p t m", t=PACK), w1s[:].rearrange("p (m t) -> p t m", t=PACK)
        )
        nc.vector.tensor_copy(y_plain[0][:, :half], y_win[0][:, :half])

        d2 = [tile(f"d2_{t}", [P, H], F32) for t in range(PACK)]
        d3 = [tile(f"d3_{t}", [P, H], F32) for t in range(PACK)]
        big = [h_win[2][:, H:]] + [tile(f"big{t}", [P, H], F32)[:] for t in range(1, PACK)]
        mix = [tile(f"mix{t}", [P, H], F32) for t in range(PACK)]
        z_bf = [tile(f"z_bf{c}", [P, hi - lo, PACK], BF16) for c, (lo, hi) in enumerate(PIECES)]
        z_q = [tile(f"z_q{c}", [P, hi - lo], U32) for c, (lo, hi) in enumerate(PIECES)]
        z_s = [tile(f"z_s{c}", [P, hi - lo], U8) for c, (lo, hi) in enumerate(PIECES)]

        def regroup(grouped, t, lo, hi, src):
            return [
                (grouped[c][:, max(a, lo) - a : min(b, hi) - a, t], src[:, max(a, lo) : min(b, hi)])
                for c, (a, b) in enumerate(PIECES)
                if max(a, lo) < min(b, hi)
            ]

        def step_d2(t, lo, hi):
            nc.vector.tensor_tensor(d2[t][:, lo:hi], looked_up(y_win[t], n2_sb, lo, hi), y_plain[t][:, lo:hi], ALU.subtract)

        def step_d3(t, lo, hi):
            nc.vector.tensor_tensor(d3[t][:, lo:hi], looked_up(y_win[t], n3_sb, lo, hi), y_plain[t][:, lo:hi], ALU.subtract)

        def step_big(t, lo, hi):
            nc.vector.tensor_tensor(big[t][:, lo:hi], d2[t][:, lo:hi], d3[t][:, lo:hi], ALU.max)

        def step_mix(t, lo, hi):
            nc.vector.tensor_tensor(mix[t][:, lo:hi], looked_up(y_win[t], n1_sb, lo, hi), big[t][:, lo:hi], ALU.subtract)
            for dst, src in regroup(z_bf, t, lo, hi, mix[t]):
                nc.scalar.activation(dst, src, COPY, scale=gt_sb[:, t : t + 1])

        def second_product(c):
            lo, hi = PIECES[c]
            quantize(z_q[c][:], z_s[c][:], z_bf[c])
            for t in range(PACK):
                nc.tensor.matmul_mx(
                    out=(y_ps if (t, c) == (0, 2) else h_ps)[t][:, lo:hi],
                    lhsT=w1w_dealt[:, 2 * P * t : 2 * P * (t + 1)].bitcast(FP4X4),
                    lhsT_scale=w1s_dealt[:, P * t : P * (t + 1)],
                    rhs=z_q[c][:].bitcast(FP8X4),
                    rhs_scale=z_s[c][:],
                    start=True,
                    stop=True,
                )

        step_d2(0, 0, H)
        step_d3(0, 0, H)
        for t in (1, 2):
            step_d2(t, 0, H)
            step_big(t - 1, 0, H)
            step_d3(t, 0, H)
            step_mix(t - 1, 0, H)
        step_d2(LAST, *HALVES[0])
        step_big(2, 0, H)
        step_d3(LAST, *HALVES[0])
        step_mix(2, 0, H)
        step_d2(LAST, *HALVES[1])
        step_big(LAST, *HALVES[0])
        step_d3(LAST, *HALVES[1])
        step_mix(LAST, *BLOCKS[0])
        step_big(LAST, *HALVES[1])
        for block in BLOCKS[1:]:
            step_mix(LAST, *block)
        for c in range(3):
            second_product(c)
        nc.scalar.copy(h_win[0][:, :split], h_ps[0][:, :split])
        nc.scalar.copy(h_win[0][:, split:H], y_ps[0][:, split:])
        for t in range(1, PACK):
            nc.scalar.copy(h_win[t][:, :H], h_ps[t][:])

        g4 = [tile(f"g4_{t}", [P, H], F32) for t in range(PACK)]
        g5 = [tile(f"g5_{t}", [P, H], F32) for t in range(PACK)]
        res_pair = [tile(f"res{u}", [P, 2, H], F32) for u in range(2)]
        res = [res_pair[t // 2][:, t % 2, :] for t in range(PACK)]
        o_bf = [tile(f"o_bf{c}", [P, hi - lo, PACK], BF16) for c, (lo, hi) in enumerate(PIECES)]
        o_q = tile("o_q", [P, H], U32)
        o_s = tile("o_s", [P, H], U8)
        out_rows = out_0.rearrange("(p t) j -> p t j", t=PACK)
        out_words = out_1[0].rearrange("p c r -> p (c r)").bitcast(I32)

        def step_g4(t, lo, hi):
            nc.vector.tensor_copy(g4[t][:, lo:hi], looked_up(h_win[t], n4_sb, lo, hi))

        def step_st(t):
            nc.vector.tensor_tensor(st_win[t][:, :H], h_ps[t][:], g4[t][:], ALU.max)

        gap = [tile(f"gap{t}", [P, H], F32) for t in range(2)]
        gain = [tile(f"gain{t}", [P, H], F32) for t in range(2)]

        def step_gain(t):
            nc.gpsimd.tensor_tensor(gap[t][:], g4[t][:], h_win[t][:, :H], ALU.subtract)
            nc.scalar.activation(gain[t][:], gap[t][:], RELU)

        def step_raise(t):
            nc.gpsimd.tensor_tensor(st_win[t][:, :H], h_win[t][:, :H], gain[t][:], ALU.add)

        def step_g5(t, lo, hi):
            nc.vector.tensor_copy(g5[t][:, lo:hi], looked_up(st_win[t], n5_sb, lo, hi))

        def step_out(t, lo, hi):
            nc.vector.tensor_tensor(res[t][:, lo:hi], st_win[t][:, lo:hi], g5[t][:, lo:hi], ALU.min)

        def round_pair(u, lo, hi):
            for c, (a, b) in enumerate(PIECES):
                if max(a, lo) < min(b, hi):
                    nc.scalar.copy(
                        o_bf[c][:, max(a, lo) - a : min(b, hi) - a, 2 * u : 2 * u + 2],
                        res_pair[u][:, :, max(a, lo) : min(b, hi)].rearrange("p e c -> p c e"),
                    )

        def store_out(t, lo, hi):
            nc.sync.dma_start(out_rows[:, t, lo:hi], res[t][:, lo:hi])

        def planes(c):
            lo, hi = PIECES[c]
            quantize(o_q[:, lo:hi], o_s[:, lo:hi], o_bf[c])

        for t in range(2):
            step_g4(t, 0, H)
            step_gain(t)
        for t in range(2):
            step_raise(t)
        step_g4(2, 0, H)
        step_g4(3, *HALVES[0])
        step_g4(3, *HALVES[1])
        step_st(2)
        step_st(3)
        step_g5(2, 0, H)
        step_g5(3, 0, H)
        step_out(2, 0, H)
        store_out(2, 0, H)
        step_out(3, 0, H)
        store_out(3, 0, H)
        round_pair(1, 0, H)
        step_g5(0, 0, H)
        step_g5(1, *BLOCKS[0])
        step_out(0, 0, H)
        store_out(0, 0, H)
        for b in range(1, 4):
            step_g5(1, *BLOCKS[b])
            step_out(1, *BLOCKS[b - 1])
            round_pair(0, *BLOCKS[b - 1])
        store_out(1, 0, split)
        step_out(1, *BLOCKS[3])
        round_pair(0, *BLOCKS[3])
        store_out(1, split, H)
        planes(0)
        planes(1)
        nc.sync.dma_start(out_words[:, :split], o_q[:, :split].bitcast(I32))
        planes(2)
        nc.sync.dma_start(out_words[:, split:], o_q[:, split:].bitcast(I32))
        for q in range(4):
            queue = nc.scalar if q % 2 else nc.sync
            queue.dma_start(out_2[0][4 * q : 4 * q + 4, :].bitcast(I32), o_s[32 * q : 32 * q + 4, :].bitcast(I32))
